import numpy as np
import ml_dtypes


def mxq(x, axis, fmt="e4m3"):
    dtype, down = {"e4m3": (ml_dtypes.float8_e4m3fn, 7), "e5m2": (ml_dtypes.float8_e5m2, 14)}[fmt]
    v = np.moveaxis(np.asarray(x, np.float32).astype(ml_dtypes.bfloat16).astype(np.float64), axis, -1)
    blocks = v.reshape(v.shape[:-1] + (-1, 32))
    amax = np.abs(blocks).max(-1, keepdims=True)
    byte = np.maximum(np.where(amax > 0, np.frexp(amax)[1] - 1 + 127, 0) - down, 1)
    scale = np.exp2(byte - 127.0)
    codes = (blocks / scale).astype(np.float32).astype(dtype).astype(np.float64)
    return np.moveaxis((codes * scale).reshape(v.shape), -1, axis)


WIDE = False


def mx_kscale(k):
    if not WIDE:
        return np.ones(k)
    levels = np.array([10, -10, 5, -5, 0])
    if k % 512:
        return np.exp2(np.random.permutation(np.resize(levels, k // 32))).repeat(32)
    a = np.empty((k // 512, 16))
    for p in range(k // 512):
        a[p, :8] = np.random.permutation(np.resize(levels, 8))
        for g in range(8):
            far = levels[np.abs(levels - a[p, g]) >= 10]
            a[p, g + 8] = far[np.random.randint(len(far))]
    return np.exp2(a.ravel()).repeat(32)


def f64(x):
    return np.asarray(x).astype(np.float64)


def striped(idx):
    return np.tile(idx.reshape(-1, 16).T, (8, 1)).astype(np.uint16)


def unstriped(offs):
    return offs[:16].T.reshape(-1).astype(np.int64)


E2M1 = np.array([0.0, 0.5, 1.0, 1.5, 2.0, 3.0, 4.0, 6.0, -0.0, -0.5, -1.0, -1.5, -2.0, -3.0, -4.0, -6.0])


def pack_weight(w, fmt):
    k, n = w.shape
    w = f64(np.asarray(w, np.float32).astype(ml_dtypes.bfloat16)).reshape(k // 32, 32, n)
    amax = np.abs(w).max(1)
    if fmt == "e4m3":
        byte = np.frexp(amax)[1] - 1 + 127 - 7
    else:
        mant, ex = np.frexp(amax / 6.0)
        byte = np.where(mant > 0.5, ex, ex - 1) + 127
    byte = np.clip(np.where(amax > 0, byte, 1), 1, 254)
    scaled = (w * np.exp2(127.0 - byte)[:, None, :]).reshape(k, n).astype(np.float32)
    by_word = np.ascontiguousarray(scaled.reshape(k // 512, 128, 4, n).transpose(0, 1, 3, 2))
    if fmt == "e4m3":
        words = by_word.astype(ml_dtypes.float8_e4m3fn).view(np.uint8)
    else:
        c = by_word.astype(ml_dtypes.float4_e2m1fn).view(np.uint8) & 0xF
        words = (c[..., 0::2] | (c[..., 1::2] << 4)).reshape(k // 512, 128, 2 * n)
    return np.ascontiguousarray(words), np.ascontiguousarray(byte.astype(np.uint8).reshape(k // 512, 16, n))


def unpack_weight(words, scales, fmt):
    g, _, n = scales.shape
    words = np.ascontiguousarray(words).reshape(g, 128, n, -1)
    if fmt == "e4m3":
        vals = words.view(ml_dtypes.float8_e4m3fn).astype(np.float64)
    else:
        nib = np.empty((g, 128, n, 4), np.uint8)
        nib[..., 0::2] = words & 0xF
        nib[..., 1::2] = words >> 4
        vals = E2M1[nib]
    vals = vals * np.repeat(np.exp2(scales.astype(np.float64) - 127.0), 8, axis=1)[..., None]
    return vals.transpose(0, 1, 3, 2).reshape(g * 512, n)


def gelu(v):
    return 0.5 * v * (1.0 + np.tanh(np.sqrt(2.0 / np.pi) * (v + 0.044715 * v**3)))


def bf(x):
    return np.asarray(x, np.float32).astype(ml_dtypes.bfloat16)


def planes(Y):
    n, m = Y.shape
    b = f64(bf(Y)).reshape(n // 32, 32, m)
    amax = np.abs(b).max(1)
    byte = np.clip(np.where(amax > 0, np.frexp(amax)[1] - 1 + 127 - 7, 1), 1, 254)
    codes = (b * np.exp2(127.0 - byte)[:, None, :]).reshape(n, m).astype(np.float32).astype(ml_dtypes.float8_e4m3fn).view(np.uint8)
    words = codes.reshape(n // 512, 128, 4, m).transpose(0, 1, 3, 2)
    return np.ascontiguousarray(words), np.ascontiguousarray(byte.astype(np.uint8).reshape(n // 512, 16, m))


T, S, T2, P, K, K2, H = 2048, 512, 2048, 1024, 1024, 512, 1024

def setup_inputs():
    n = np.random.standard_normal
    s, s2, u = mx_kscale(K)[:, None], mx_kscale(K2)[:, None], mx_kscale(H)[:, None]
    perm = np.random.permutation(T2)
    d = {}
    d["tab_words"], d["tab_scales"] = pack_weight(n((K, T)) * s, "e4m3")
    d["tab2_words"], d["tab2_scales"] = pack_weight(n((K2, T)) * s2, "e4m3")
    d["offs"] = striped(np.random.permutation(T)[:S])
    d["offs2"] = striped(np.random.permutation(T)[:S])
    d["offs3"] = striped(perm[:S])
    d["offs4"] = striped(perm[S:2 * S])
    d["offs5"] = striped(np.random.permutation(T2)[:P])
    d["wl"] = (n((K, H)) * 0.75 / K ** 0.5 / s).astype(np.float32)
    d["wc_words"], d["wc_scales"] = pack_weight(n((K, H)) * 0.55 / K ** 0.5 / s, "e4m3")
    d["wm_words"], d["wm_scales"] = pack_weight(n((K2, H)) * 1.3 / K2 ** 0.5 / s2, "e2m1")
    d["gm"] = (0.7 * np.exp(0.3 * n(H))).astype(np.float32)
    d["wg1"] = np.exp(0.3 * n((128, S))).astype(np.float32)
    d["wg2"] = np.exp(0.3 * n((128, S))).astype(np.float32)
    d["page0"] = (0.4 * n((H, T2))).astype(np.float32)
    d["gz"] = (np.exp(0.3 * n(H)) * u[:, 0]).astype(np.float32)
    d["wo"] = (n((H, H)) * 0.8 * np.exp(0.8 * n(H)) / H ** 0.5 / u).astype(np.float32)
    return d

def reference(tab_words, tab_scales, tab2_words, tab2_scales, offs, offs2, offs3, offs4, offs5,
              wl, wc_words, wc_scales, wm_words, wm_scales, gm, wg1, wg2, page0, gz, wo):
    v = unpack_weight(tab_words, tab_scales, "e4m3")[:, unstriped(offs)]
    v2 = unpack_weight(tab2_words, tab2_scales, "e4m3")[:, unstriped(offs2)]
    shoot = mxq(f64(wl), 0, "e4m3").T @ v
    curl = unpack_weight(wc_words, wc_scales, "e4m3").T @ v
    h1 = np.minimum(shoot, np.sin(curl))
    moist = unpack_weight(wm_words, wm_scales, "e2m1").T @ v2
    h2 = f64(gm)[:, None] * np.tanh(moist)
    page = f64(page0).copy()
    page[:, unstriped(offs3)] = np.tile(f64(wg1), (H // 128, 1)) * h1
    page[:, unstriped(offs4)] = np.tile(f64(wg2), (H // 128, 1)) * h2
    z = np.abs(page[:, unstriped(offs5)])
    x = f64(gz)[:, None] * z
    y = (mxq(f64(wo), 0, "e4m3").T @ mxq(x, 0, "e4m3")) + z
    words, scales = planes(y)
    return y, words, scales

@@ -1,0 +1,380 @@
+import math
+from contextlib import ExitStack
+
+import concourse.mybir as mybir
+from concourse.masks import make_identity
+
+T, S, T2, NJ, K, K2, H = 2048, 512, 2048, 1024, 1024, 512, 1024
+FLOPS = 2 * K * H * S * 2 + 2 * K2 * H * S + 2 * H * H * NJ
+
+F32 = mybir.dt.float32
+BF16 = mybir.dt.bfloat16
+I32 = mybir.dt.int32
+U32 = mybir.dt.uint32
+U16 = mybir.dt.uint16
+U8 = mybir.dt.uint8
+FP8X4 = mybir.dt.float8_e4m3fn_x4
+FP4X4 = mybir.dt.float4_e2m1fn_x4
+ACT = mybir.ActivationFunctionType
+ALU = mybir.AluOpType
+
+P = 128
+PACK = 4
+PASS = P * PACK
+QUADS = 4
+TURN = 2.0 * math.pi
+ROUND = 1.5 * 2.0**23
+
+
+def tile_list_bonsai_branch_slots_kernel(
+    tc, tab_words, tab_scales, tab2_words, tab2_scales, offs, offs2, offs3, offs4, offs5,
+    wl, wc_words, wc_scales, wm_words, wm_scales, gm, wg1, wg2, page0, gz, wo,
+    out_0, out_1, out_2,
+):
+    nc = tc.nc
+    slices = [(b, t) for b in range(2) for t in range(PACK)]
+
+    with ExitStack() as ctx:
+        lists = ctx.enter_context(tc.tile_pool(name="lists", bufs=1))
+        sb = ctx.enter_context(tc.tile_pool(name="sb", bufs=1))
+        psum = ctx.enter_context(tc.psum_pool(name="psum", bufs=8))
+
+        def tile(shape, dtype, name, tag=None, bufs=1):
+            return sb.tile(shape, dtype, name=name, tag=tag or name, bufs=bufs, align_bytes=64)
+
+        def bank(name):
+            return psum.tile([P, PASS], F32, name=name, tag="bank")
+
+        def load_list(src, name):
+            lst = lists.tile(list(src.shape), U16, name=name)
+            nc.sync.dma_start(lst[:], src)
+            return lst
+
+        def load_words(src, name, tag):
+            words = src.rearrange("p n t -> p (n t)").bitcast(I32)
+            dst = tile(list(words.shape), I32, name, tag)
+            nc.sync.dma_start(dst[:], words)
+            return dst
+
+        def load_plane_repeated(queue, src, name):
+            dst = tile([P, src.shape[2]], U8, name)
+            for q in range(QUADS):
+                rows = src[0, 4 * q : 4 * q + 4, :].bitcast(I32)
+                queue.dma_start(dst[32 * q : 32 * q + 32, :].bitcast(I32), rows.partition_broadcast(8))
+            return dst
+
+        def load_planes(src, name):
+            dst = tile([P, src.shape[2]], U8, name)
+            rows = 4 * src.shape[0]
+            nc.gpsimd.memset(dst[:].bitcast(I32), 0)
+            for q in range(QUADS):
+                nc.gpsimd.dma_start(
+                    dst[32 * q : 32 * q + rows, :].bitcast(I32), src[:, 4 * q : 4 * q + 4, :].bitcast(I32)
+                )
+            return dst
+
+        def load_gate(src, t0, t1, name):
+            dst = tile([P, t1 - t0, S], F32, name)
+            for q in range(QUADS):
+                nc.sync.dma_start(dst[32 * q : 32 * q + 32, :, :], src.rearrange("(q t) s -> q t s", t=PACK)[:, t0:t1, :])
+            return [dst[:, t, :] for t in range(t1 - t0)]
+
+        def load_factor(src, name):
+            dst = tile([P, 2, PACK], F32, name)
+            nc.gpsimd.dma_start(dst[:], src.rearrange("(b p t) -> p b t", b=2, t=PACK))
+            return dst
+
+        page_rows = page0.rearrange("(b p t) c -> b t p c", b=2, t=PACK)
+        pages = {}
+
+        def load_page(s):
+            b, t = slices[s]
+            pages[b, t] = tile([P, T2], F32, "page%d" % s)
+            nc.sync.dma_start(pages[b, t][:], page_rows[b, t])
+
+        def load_weight(src, a, g, name, tag):
+            raw = tile([P, PACK, PASS], F32, name, tag)
+            rows = src[PASS * a : PASS * (a + 1), PASS * g : PASS * (g + 1)]
+            nc.sync.dma_start(raw[:], rows.rearrange("(p i) c -> p i c", i=PACK))
+            return raw
+
+        def quantize(grouped, name, tag):
+            codes = tile([P, PASS], U32, name, tag)
+            scales = tile([P, PASS], U8, name + "s", tag + "s")
+            nc.vector.quantize_mx(out=codes[:].bitcast(FP8X4), scales=scales[:], in_=grouped[:])
+            return codes, scales
+
+        def quantize_weight(raw, name, tag):
+            grouped = tile([P, PACK * PASS], BF16, name + "b", "grouped", bufs=4)
+            nc.scalar.copy(
+                out=grouped[:].rearrange("p (t m i) -> p m t i", t=PACK, i=PACK),
+                in_=raw[:].rearrange("p i (m t) -> p m t i", t=PACK),
+            )
+            return quantize(grouped, name, tag)
+
+        def interleave(shares, src, name):
+            grouped = tile([P, PACK * PASS], BF16, name, "grouped", bufs=4)
+            width = P // len(shares)
+            for n, copy in enumerate(shares):
+                copy(
+                    out=grouped[:].rearrange("p (c i t) -> p c t i", t=PACK, i=4)[:, width * n : width * (n + 1)],
+                    in_=src[:].rearrange("p t (c i) -> p c t i", i=4)[:, width * n : width * (n + 1)],
+                )
+            return grouped
+
+        def gather(window, lst, dtype, name):
+            picked = tile([P, S], dtype, name)
+            nc.vector.tensor_copy(picked[:], window[:].bitcast(dtype).indirect(lst[:]))
+            return picked
+
+        warm = tile([P, 8], F32, "warm")
+        nc.vector.memset(warm[:], 0.0)
+        nc.scalar.activation(warm[:], warm[:], ACT.Silu)
+        wm_raw = tile([P, 2 * H], U8, "wm_raw")
+        nc.sync.dma_start(wm_raw[:].bitcast(I32), wm_words[0].bitcast(I32))
+        tab2w = load_words(tab2_words[0], "tab2w", "C")
+        idx2 = load_list(offs2, "idx2")
+        tab2s = load_plane_repeated(nc.sync, tab2_scales, "tab2s")
+        wms_raw = load_planes(wm_scales, "wms_raw")
+        gm_sb = load_factor(gm, "gm_sb")
+        tabs = load_planes(tab_scales, "tabs")
+        wcs = load_planes(wc_scales, "wcs")
+        ident = tile([P, P], F32, "ident")
+        make_identity(nc, ident[:])
+        gz_sb = load_factor(gz, "gz_sb")
+        wg2_sb = load_gate(wg2, 0, 2, "wg2a")
+        idx4 = load_list(offs4, "idx4")
+        load_page(0)
+        load_page(1)
+        idx = load_list(offs, "idx")
+        tabw = [load_words(tab_words[a], "tabw%d" % a, "AB"[a]) for a in range(2)]
+        load_page(4)
+        wcw = [load_words(wc_words[a], "wcw%d" % a, "wcw%d" % a) for a in range(2)]
+        load_page(5)
+        wg2_sb += load_gate(wg2, 2, 4, "wg2b")
+        load_page(2)
+        wl_raw = {}
+        wl_raw[0, 0] = load_weight(wl, 0, 0, "wl00", "D")
+        load_page(3)
+        wl_raw[1, 0] = load_weight(wl, 1, 0, "wl10", "E")
+        load_page(6)
+        idx3 = load_list(offs3, "idx3")
+        wg1_sb = load_gate(wg1, 0, 4, "wg1_sb")
+        idx5 = load_list(offs5, "idx5")
+        load_page(7)
+
+        wm_deal = tile([P, 2 * H], U8, "wm_deal")
+        nc.vector.tensor_copy(
+            wm_deal[:].bitcast(U16).rearrange("p (g t m) -> p g t m", g=2, t=PACK),
+            wm_raw[:].bitcast(U16).rearrange("p (g m t) -> p g t m", g=2, t=PACK),
+        )
+        wms_deal = tile([P, H], U8, "wms_deal")
+        nc.vector.tensor_copy(
+            wms_deal[:].rearrange("p (g t m) -> p g t m", g=2, t=PACK),
+            wms_raw[:].rearrange("p (g m t) -> p g t m", g=2, t=PACK),
+        )
+        v2w = gather(tab2w, idx2, U32, "v2w")
+        v2s = gather(tab2s, idx2, U8, "v2s")
+        h2 = {}
+        gate1 = {(b, t): wg1_sb[t] for b, t in slices}
+        gate2 = {}
+        for s, (b, t) in enumerate(slices):
+            gate2[b, t] = tile([P, S], F32, "gate2_%d" % t)[:] if b == 0 else wg2_sb[t]
+            nc.scalar.activation(gate2[b, t], wg2_sb[t], ACT.Copy, scale=gm_sb[:, b, t : t + 1])
+            moist = bank("moist%d" % s)
+            nc.tensor.matmul_mx(
+                out=moist[:],
+                lhsT=wm_deal[:, 2 * P * s : 2 * P * (s + 1)].bitcast(FP4X4),
+                lhsT_scale=wms_deal[:, P * s : P * (s + 1)],
+                rhs=v2w[:].bitcast(FP8X4),
+                rhs_scale=v2s[:],
+                start=True,
+                stop=True,
+            )
+            h2[b, t] = tile([P, S], F32, "h2_%d" % s, "row", bufs=12)
+            nc.scalar.activation(h2[b, t][:], moist[:], ACT.Tanh)
+
+        def put(lst, values, gate, b, t):
+            nc.vector.tensor_tensor(pages[b, t][:].indirect(lst[:]), values[:], gate[b, t], ALU.mult)
+
+        put(idx4, h2[0, 0], gate2, 0, 0)
+        put(idx4, h2[0, 1], gate2, 0, 1)
+        vw = [gather(tabw[a], idx, U32, "vw%d" % a) for a in range(2)]
+        vs = gather(tabs, idx, U8, "vs")
+        for a in range(2):
+            wl_raw[a, 1] = load_weight(wl, a, 1, "wl%d1" % a, "AB"[a])
+
+        sins = {}
+
+        def curl_half(g):
+            turns = tile([P, 4, PACK, P], F32, "turns%d" % g, "G")
+            whole = tile([P, 4, PACK, P], F32, "whole%d" % g, "H")
+            for jb in range(4):
+                curl = bank("curl%d%d" % (g, jb))
+                for a in range(2):
+                    nc.tensor.matmul_mx(
+                        out=curl[:],
+                        lhsT=vw[a][:, P * jb : P * (jb + 1)].bitcast(FP8X4),
+                        lhsT_scale=vs[4 * a :, P * jb : P * (jb + 1)],
+                        rhs=wcw[a][:, PASS * g : PASS * (g + 1)].bitcast(FP8X4),
+                        rhs_scale=wcs[4 * a :, PASS * g : PASS * (g + 1)],
+                        start=(a == 0),
+                        stop=(a == 1),
+                    )
+                nc.scalar.activation(
+                    turns[:, jb, :, :], curl[:].rearrange("p (m t) -> p t m", t=PACK), ACT.Copy, scale=1.0 / TURN
+                )
+                nearest = tile([P, PACK, P], U32, "nearest%d%d" % (g, jb), "nearest", bufs=2)
+                nc.scalar.activation(nearest[:], turns[:, jb, :, :], ACT.Copy, bias=ROUND)
+                nc.scalar.activation(whole[:, jb, :, :], nearest[:], ACT.Copy, scale=-1.0, bias=ROUND)
+            for t in range(PACK):
+                rest = bank("rest%d%d" % (g, t))
+                for jb in range(4):
+                    for n, part in enumerate((turns, whole)):
+                        nc.tensor.matmul(
+                            rest[:, P * jb : P * (jb + 1)], part[:, jb, t, :], ident[:],
+                            start=(n == 0), stop=(n == 1), is_transpose=True,
+                        )
+                sins[g, t] = tile([P, S], F32, "sin%d%d" % (g, t), "row", bufs=12)
+                nc.scalar.activation(sins[g, t][:], rest[:], ACT.Sin, scale=TURN)
+
+        for b, t in slices[2:6]:
+            put(idx4, h2[b, t], gate2, b, t)
+
+        picked = {}
+
+        def shoot_half(g, wlq):
+            for t in range(PACK):
+                shoot = bank("shoot%d%d" % (g, t))
+                for a in range(2):
+                    codes, scales = wlq[a]
+                    nc.tensor.matmul_mx(
+                        out=shoot[:],
+                        lhsT=codes[:, P * t : P * (t + 1)].bitcast(FP8X4),
+                        lhsT_scale=scales[:, P * t : P * (t + 1)],
+                        rhs=vw[a][:].bitcast(FP8X4),
+                        rhs_scale=vs[4 * a :, :],
+                        start=(a == 0),
+                        stop=(a == 1),
+                    )
+                nc.vector.tensor_tensor(sins[g, t][:], shoot[:], sins[g, t][:], ALU.min)
+                put(idx3, sins[g, t], gate1, g, t)
+                if g == 1 and t < 2:
+                    pick(1, t, 0)
+                    pick(1, t, 1)
+
+        z = {}
+
+        def pick(b, t, h):
+            picked[b, t, h] = z[b, h][:, t, :]
+            cols = PASS // 16
+            nc.vector.tensor_copy(picked[b, t, h], pages[b, t][:].indirect(idx5[:, cols * h : cols * (h + 1)]))
+
+        wlq = [quantize_weight(wl_raw[a, 0], "wlq%d0" % a, "q%d" % a) for a in range(2)]
+        curl_half(0)
+        shoot_half(0, wlq)
+        for b, t in slices[6:]:
+            put(idx4, h2[b, t], gate2, b, t)
+        wlq = [quantize_weight(wl_raw[a, 1], "wlq%d1" % a, "q%d" % (2 + a)) for a in range(2)]
+        curl_half(1)
+        woq = {}
+        for b in range(2):
+            for g in range(2):
+                raw = load_weight(wo, b, g, "wo%d%d" % (b, g), "DEAB"[2 * b + g])
+                woq[b, g] = quantize_weight(raw, "woq%d%d" % (b, g), "woq%d%d" % (b, g))
+        for b in range(2):
+            for h in range(2):
+                z[b, h] = tile([P, PACK, PASS], F32, "z%d%d" % (b, h), "DEAB"[2 * b + h])
+        for h in range(2):
+            for t in range(PACK):
+                pick(0, t, h)
+        shoot_half(1, wlq)
+        for h in range(2):
+            for t in range(2, PACK):
+                pick(1, t, h)
+
+        xq = {}
+
+        xb = {}
+        for b in range(2):
+            for h in range(2):
+                xb[b, h] = tile([P, PACK, PASS], BF16, "xb%d%d" % (b, h), ("G", "H", "C", "wg2a")[2 * b + h])
+
+        def absolute(b, t, h):
+            nc.scalar.activation(z[b, h][:, t, :], z[b, h][:, t, :], ACT.Abs)
+
+        def scale(b, t, h, out):
+            nc.scalar.activation(out, z[b, h][:, t, :], ACT.Copy, scale=gz_sb[:, b, t : t + 1])
+
+        def quantize_x(b, h):
+            grouped = interleave((nc.scalar.copy,), xb[b, h], "xi%d%d" % (b, h))
+            xq[b, h] = quantize(grouped, "xq%d%d" % (b, h), "q%d" % (2 * b + h))
+
+        for h in range(2):
+            for t in range(PACK):
+                absolute(0, t, h)
+            if h == 1:
+                quantize_x(0, 0)
+            for t in range(PACK):
+                scale(0, t, h, xb[0, h][:, t, :])
+        xi = [tile([P, PACK * PASS], BF16, "xi1%d" % h, "grouped", bufs=4) for h in range(2)]
+
+        def weave(copy, h, ts):
+            copy(
+                out=xi[h][:].rearrange("p (c i t) -> p c t i", t=PACK, i=4)[:, :, ts, :],
+                in_=xb[1, h][:].rearrange("p t (c i) -> p c t i", i=4)[:, :, ts, :],
+            )
+
+        for t in range(2):
+            for h in range(2):
+                absolute(1, t, h)
+            if t == 0:
+                quantize_x(0, 1)
+            for h in range(2):
+                scale(1, t, h, xb[1, h][:, t, :])
+        for h in range(2):
+            weave(nc.scalar.copy, h, slice(0, 2))
+        for h in range(2):
+            for t in range(2, PACK):
+                absolute(1, t, h)
+            for t in range(2, PACK):
+                scale(1, t, h, xb[1, h][:, t, :])
+            weave(nc.vector.tensor_copy, h, slice(2, PACK))
+            xq[1, h] = quantize(xi[h], "xq1%d" % h, "q%d" % (2 + h))
+
+        y_rows = out_0.rearrange("(g p t) j -> g t p j", g=2, t=PACK)
+        y_codes = [tile([P, NJ], U32, "ycodes%d" % g, "wcw%d" % g) for g in range(2)]
+        y_scales = tile([P, 2 * NJ], U8, "yscales", "tabs")
+        for h in range(2):
+            cols = slice(PASS * h, PASS * (h + 1))
+            for g in range(2):
+                for t in range(PACK):
+                    acc = bank("acc%d%d%d" % (h, g, t))
+                    for b in range(2):
+                        nc.tensor.matmul_mx(
+                            out=acc[:],
+                            lhsT=woq[b, g][0][:, P * t : P * (t + 1)].bitcast(FP8X4),
+                            lhsT_scale=woq[b, g][1][:, P * t : P * (t + 1)],
+                            rhs=xq[b, h][0][:].bitcast(FP8X4),
+                            rhs_scale=xq[b, h][1][:],
+                            start=(b == 0),
+                            stop=(b == 1),
+                        )
+                    y = z[g, h][:, t, :]
+                    nc.vector.tensor_tensor(y, acc[:], y, ALU.add)
+                    nc.sync.dma_start(y_rows[g, t][:, cols], y)
+                shares = (nc.scalar.copy, nc.vector.tensor_copy) if (g, h) == (1, 1) else (nc.scalar.copy,)
+                grouped = interleave(shares, z[g, h], "yi%d%d" % (g, h))
+                nc.vector.quantize_mx(
+                    out=y_codes[g][:, cols].bitcast(FP8X4),
+                    scales=y_scales[:, NJ * g + PASS * h : NJ * g + PASS * (h + 1)],
+                    in_=grouped[:],
+                )
+                nc.sync.dma_start(
+                    out_1[g].rearrange("p m t -> p (m t)").bitcast(I32)[:, cols], y_codes[g][:, cols].bitcast(I32)
+                )
+        for q in range(QUADS):
+            nc.sync.dma_start(
+                out_2.bitcast(I32)[:, 4 * q : 4 * q + 4, :].rearrange("g r m -> r g m"),
+                y_scales[32 * q : 32 * q + 4, :].bitcast(I32).rearrange("r (g m) -> r g m", g=2),
+            )

@@ -4,7 +4,7 @@ from contextlib import ExitStack
 import concourse.mybir as mybir
 from concourse.masks import make_identity
 
-T, S, T2, NJ, K, K2, H = 2048, 512, 2048, 1024, 1024, 512, 1024
+S, T2, NJ, K, K2, H = 512, 2048, 1024, 1024, 512, 1024
 FLOPS = 2 * K * H * S * 2 + 2 * K2 * H * S + 2 * H * H * NJ
 
 F32 = mybir.dt.float32
@@ -21,9 +21,14 @@ ALU = mybir.AluOpType
 P = 128
 PACK = 4
 PASS = P * PACK
-QUADS = 4
+QUAD = 32
+QUADS = P // QUAD
+LIVE = 4
+BLOCKS = S // P
+RUN = 4
 TURN = 2.0 * math.pi
 ROUND = 1.5 * 2.0**23
+SCALAR_RUNS = 48
 
 
 def tile_list_bonsai_branch_slots_kernel(
@@ -37,344 +42,382 @@ def tile_list_bonsai_branch_slots_kernel(
     with ExitStack() as ctx:
         lists = ctx.enter_context(tc.tile_pool(name="lists", bufs=1))
         sb = ctx.enter_context(tc.tile_pool(name="sb", bufs=1))
-        psum = ctx.enter_context(tc.psum_pool(name="psum", bufs=8))
+        psum = ctx.enter_context(tc.psum_pool(name="psum", bufs=1))
 
-        def tile(shape, dtype, name, tag=None, bufs=1):
-            return sb.tile(shape, dtype, name=name, tag=tag or name, bufs=bufs, align_bytes=64)
+        def tile(shape, dtype, name, tag=None):
+            return sb.tile(shape, dtype, name=name, tag=tag or name, align_bytes=64)
 
-        def bank(name):
-            return psum.tile([P, PASS], F32, name=name, tag="bank")
+        def bank(name, n):
+            return psum.tile([P, PASS], F32, name=name, tag="bank%d" % n)
 
         def load_list(src, name):
             lst = lists.tile(list(src.shape), U16, name=name)
             nc.sync.dma_start(lst[:], src)
             return lst
 
-        def load_words(src, name, tag):
-            words = src.rearrange("p n t -> p (n t)").bitcast(I32)
-            dst = tile(list(words.shape), I32, name, tag)
-            nc.sync.dma_start(dst[:], words)
+        def load(src, dtype, name, tag=None):
+            dst = tile(list(src.shape), dtype, name, tag)
+            nc.sync.dma_start(dst[:], src)
             return dst
 
-        def load_plane_repeated(queue, src, name):
-            dst = tile([P, src.shape[2]], U8, name)
-            for q in range(QUADS):
-                rows = src[0, 4 * q : 4 * q + 4, :].bitcast(I32)
-                queue.dma_start(dst[32 * q : 32 * q + 32, :].bitcast(I32), rows.partition_broadcast(8))
-            return dst
+        def as_words(src):
+            return src.rearrange("p n i -> p (n i)").bitcast(I32)
 
-        def load_planes(src, name):
+        def zeroed_planes(src, name):
             dst = tile([P, src.shape[2]], U8, name)
-            rows = 4 * src.shape[0]
             nc.gpsimd.memset(dst[:].bitcast(I32), 0)
-            for q in range(QUADS):
-                nc.gpsimd.dma_start(
-                    dst[32 * q : 32 * q + rows, :].bitcast(I32), src[:, 4 * q : 4 * q + 4, :].bitcast(I32)
+            return dst
+
+        def load_plane(dst, src):
+            for r in range(LIVE):
+                nc.sync.dma_start(dst[r:P:QUAD, :].bitcast(I32), src[0, r : LIVE * QUADS : LIVE, :].bitcast(I32))
+
+        def load_two_planes(src, name):
+            dst = zeroed_planes(src, name)
+            for quad in range(QUADS):
+                nc.sync.dma_start(
+                    dst[QUAD * quad : QUAD * quad + 2 * LIVE, :].bitcast(I32),
+                    src[:, LIVE * quad : LIVE * (quad + 1), :].bitcast(I32),
                 )
             return dst
 
-        def load_gate(src, t0, t1, name):
-            dst = tile([P, t1 - t0, S], F32, name)
-            for q in range(QUADS):
-                nc.sync.dma_start(dst[32 * q : 32 * q + 32, :, :], src.rearrange("(q t) s -> q t s", t=PACK)[:, t0:t1, :])
-            return [dst[:, t, :] for t in range(t1 - t0)]
-
         def load_factor(src, name):
-            dst = tile([P, 2, PACK], F32, name)
-            nc.gpsimd.dma_start(dst[:], src.rearrange("(b p t) -> p b t", b=2, t=PACK))
-            return dst
+            return load(src.rearrange("(b p t) -> p b t", b=2, t=PACK), F32, name)
 
         page_rows = page0.rearrange("(b p t) c -> b t p c", b=2, t=PACK)
         pages = {}
 
-        def load_page(s):
-            b, t = slices[s]
-            pages[b, t] = tile([P, T2], F32, "page%d" % s)
-            nc.sync.dma_start(pages[b, t][:], page_rows[b, t])
+        def load_page(b, t):
+            pages[b, t] = load(page_rows[b, t], F32, "page%d%d" % (b, t))
 
         def load_weight(src, a, g, name, tag):
-            raw = tile([P, PACK, PASS], F32, name, tag)
             rows = src[PASS * a : PASS * (a + 1), PASS * g : PASS * (g + 1)]
-            nc.sync.dma_start(raw[:], rows.rearrange("(p i) c -> p i c", i=PACK))
-            return raw
+            return load(rows.rearrange("(p i) c -> p i c", i=PACK), F32, name, tag)
 
-        def quantize(grouped, name, tag):
-            codes = tile([P, PASS], U32, name, tag)
-            scales = tile([P, PASS], U8, name + "s", tag + "s")
-            nc.vector.quantize_mx(out=codes[:].bitcast(FP8X4), scales=scales[:], in_=grouped[:])
-            return codes, scales
-
-        def quantize_weight(raw, name, tag):
-            grouped = tile([P, PACK * PASS], BF16, name + "b", "grouped", bufs=4)
-            nc.scalar.copy(
-                out=grouped[:].rearrange("p (t m i) -> p m t i", t=PACK, i=PACK),
-                in_=raw[:].rearrange("p i (m t) -> p m t i", t=PACK),
-            )
-            return quantize(grouped, name, tag)
-
-        def interleave(shares, src, name):
-            grouped = tile([P, PACK * PASS], BF16, name, "grouped", bufs=4)
-            width = P // len(shares)
-            for n, copy in enumerate(shares):
-                copy(
-                    out=grouped[:].rearrange("p (c i t) -> p c t i", t=PACK, i=4)[:, width * n : width * (n + 1)],
-                    in_=src[:].rearrange("p t (c i) -> p c t i", i=4)[:, width * n : width * (n + 1)],
-                )
-            return grouped
+        def load_wc(g):
+            words = wc_words.rearrange("a p n i -> p a (n i)").bitcast(I32)
+            return load(words[:, :, PASS * g : PASS * (g + 1)], I32, "wcw%d" % g)
 
         def gather(window, lst, dtype, name):
             picked = tile([P, S], dtype, name)
             nc.vector.tensor_copy(picked[:], window[:].bitcast(dtype).indirect(lst[:]))
             return picked
 
+        def quantize(woven, name, tag):
+            codes = tile([P, PASS], U32, name, tag)
+            scales = tile([P, PASS], U8, name + "s", tag + "s")
+            nc.vector.quantize_mx(out=codes[:].bitcast(FP8X4), scales=scales[:], in_=woven[:])
+            return codes[:], scales[:]
+
+        def weave_weight(raw, name, tag):
+            woven = tile([P, PACK * PASS], BF16, name, tag)
+            nc.scalar.copy(
+                out=woven[:].rearrange("p (t m i) -> p m t i", t=PACK, i=PACK),
+                in_=raw[:].rearrange("p i (m t) -> p m t i", t=PACK),
+            )
+            return woven
+
+        def weave(copy, woven, src, runs=slice(0, PASS // RUN), ts=slice(0, PACK)):
+            copy(
+                out=woven[:].rearrange("p (u e t) -> p u t e", t=PACK, e=RUN)[:, runs, ts, :],
+                in_=src[:].rearrange("p t (u e) -> p u t e", e=RUN)[:, runs, ts, :],
+            )
+
+        def two_passes(out, stationary, moving):
+            for a in range(2):
+                nc.tensor.matmul_mx(
+                    out=out[:],
+                    lhsT=stationary[a][0].bitcast(FP8X4),
+                    lhsT_scale=stationary[a][1],
+                    rhs=moving[a][0].bitcast(FP8X4),
+                    rhs_scale=moving[a][1],
+                    start=(a == 0),
+                    stop=(a == 1),
+                )
+
+        def columns(operand, n):
+            return [(codes[:, P * n : P * (n + 1)], scales[:, P * n : P * (n + 1)]) for codes, scales in operand]
+
+        def spread_gate(rows, name, tag):
+            turned = bank(name + "_turned", 7)
+            for jb in range(BLOCKS):
+                nc.tensor.transpose(turned[:, P * jb : P * (jb + 1)], rows[:, P * jb : P * (jb + 1)], ident[:])
+            repeated = tile([P, PACK, BLOCKS, QUADS, QUAD], F32, name + "_repeated", tag)
+            by_t = turned[:].rearrange("p (jb m t) -> p t jb m", jb=BLOCKS, t=PACK)
+
+            def gate_bank(t):
+                nc.scalar.copy(repeated[:, t], by_t[:, t].unsqueeze(2).to_broadcast([P, BLOCKS, QUADS, QUAD]))
+                back = bank("%s_back%d" % (name, t), 3 + t)
+                for jb in range(BLOCKS):
+                    nc.tensor.transpose(
+                        back[:, P * jb : P * (jb + 1)], repeated[:, t, jb].rearrange("p q m -> p (q m)"), ident[:]
+                    )
+                return back
+
+            return gate_bank
+
+        def put(lst, values, gate, b, t):
+            nc.vector.tensor_tensor(pages[b, t][:].indirect(lst[:]), values[:], gate, ALU.mult)
+
         warm = tile([P, 8], F32, "warm")
         nc.vector.memset(warm[:], 0.0)
         nc.scalar.activation(warm[:], warm[:], ACT.Silu)
+
+        wg2_rows = load(wg2, F32, "wg2_rows", "nearest0")
+        idx2 = load_list(offs2, "idx2")
+        tab2s = zeroed_planes(tab2_scales, "tab2s")
+        load_plane(tab2s, tab2_scales)
         wm_raw = tile([P, 2 * H], U8, "wm_raw")
         nc.sync.dma_start(wm_raw[:].bitcast(I32), wm_words[0].bitcast(I32))
-        tab2w = load_words(tab2_words[0], "tab2w", "C")
-        idx2 = load_list(offs2, "idx2")
-        tab2s = load_plane_repeated(nc.sync, tab2_scales, "tab2s")
-        wms_raw = load_planes(wm_scales, "wms_raw")
+        tab2w = load(as_words(tab2_words[0]), I32, "tab2w", "big2")
+        wms_raw = zeroed_planes(wm_scales, "wms_raw")
+        load_plane(wms_raw, wm_scales)
         gm_sb = load_factor(gm, "gm_sb")
-        tabs = load_planes(tab_scales, "tabs")
-        wcs = load_planes(wc_scales, "wcs")
+        idx4 = load_list(offs4, "idx4")
+        load_page(0, 0)
+        load_page(0, 1)
+        wg1_rows = load(wg1, F32, "wg1_rows", "nearest1")
+        idx = load_list(offs, "idx")
+        tabs = load_two_planes(tab_scales, "tabs")
+        tabw = [load(as_words(tab_words[a]), I32, "tabw%d" % a, "big%d" % a) for a in range(2)]
+        load_page(0, 2)
+        wcw = [load_wc(0)]
+        wcs = load_two_planes(wc_scales, "wcs")
+        load_page(0, 3)
+        load_page(1, 0)
         ident = tile([P, P], F32, "ident")
         make_identity(nc, ident[:])
-        gz_sb = load_factor(gz, "gz_sb")
-        wg2_sb = load_gate(wg2, 0, 2, "wg2a")
-        idx4 = load_list(offs4, "idx4")
-        load_page(0)
-        load_page(1)
-        idx = load_list(offs, "idx")
-        tabw = [load_words(tab_words[a], "tabw%d" % a, "AB"[a]) for a in range(2)]
-        load_page(4)
-        wcw = [load_words(wc_words[a], "wcw%d" % a, "wcw%d" % a) for a in range(2)]
-        load_page(5)
-        wg2_sb += load_gate(wg2, 2, 4, "wg2b")
-        load_page(2)
-        wl_raw = {}
-        wl_raw[0, 0] = load_weight(wl, 0, 0, "wl00", "D")
-        load_page(3)
-        wl_raw[1, 0] = load_weight(wl, 1, 0, "wl10", "E")
-        load_page(6)
-        idx3 = load_list(offs3, "idx3")
-        wg1_sb = load_gate(wg1, 0, 4, "wg1_sb")
-        idx5 = load_list(offs5, "idx5")
-        load_page(7)
 
-        wm_deal = tile([P, 2 * H], U8, "wm_deal")
+        v2s = gather(tab2s, idx2, U8, "v2s")
+        wm_dealt = tile([P, 2 * H], U8, "wm_dealt")
         nc.vector.tensor_copy(
-            wm_deal[:].bitcast(U16).rearrange("p (g t m) -> p g t m", g=2, t=PACK),
-            wm_raw[:].bitcast(U16).rearrange("p (g m t) -> p g t m", g=2, t=PACK),
-        )
-        wms_deal = tile([P, H], U8, "wms_deal")
-        nc.vector.tensor_copy(
-            wms_deal[:].rearrange("p (g t m) -> p g t m", g=2, t=PACK),
-            wms_raw[:].rearrange("p (g m t) -> p g t m", g=2, t=PACK),
+            wm_dealt[:].bitcast(U16).rearrange("p (b t m) -> p b t m", b=2, t=PACK),
+            wm_raw[:].bitcast(U16).rearrange("p (b m t) -> p b t m", b=2, t=PACK),
         )
         v2w = gather(tab2w, idx2, U32, "v2w")
-        v2s = gather(tab2s, idx2, U8, "v2s")
-        h2 = {}
-        gate1 = {(b, t): wg1_sb[t] for b, t in slices}
-        gate2 = {}
-        for s, (b, t) in enumerate(slices):
-            gate2[b, t] = tile([P, S], F32, "gate2_%d" % t)[:] if b == 0 else wg2_sb[t]
-            nc.scalar.activation(gate2[b, t], wg2_sb[t], ACT.Copy, scale=gm_sb[:, b, t : t + 1])
-            moist = bank("moist%d" % s)
+        wms_dealt = tile([P, H], U8, "wms_dealt")
+        for b in range(2):
+            nc.vector.tensor_copy(
+                wms_dealt[:].rearrange("p (b t m) -> p b t m", b=2, t=PACK)[:, b],
+                wms_raw[:].rearrange("p (b m t) -> p b t m", b=2, t=PACK)[:, b],
+            )
+
+        tanhs = {}
+
+        def moist_slice(b, t):
+            s = PACK * b + t
+            moist = bank("moist%d" % s, s % 3)
             nc.tensor.matmul_mx(
                 out=moist[:],
-                lhsT=wm_deal[:, 2 * P * s : 2 * P * (s + 1)].bitcast(FP4X4),
-                lhsT_scale=wms_deal[:, P * s : P * (s + 1)],
+                lhsT=wm_dealt[:, 2 * P * s : 2 * P * (s + 1)].bitcast(FP4X4),
+                lhsT_scale=wms_dealt[:, P * s : P * (s + 1)],
                 rhs=v2w[:].bitcast(FP8X4),
                 rhs_scale=v2s[:],
                 start=True,
                 stop=True,
             )
-            h2[b, t] = tile([P, S], F32, "h2_%d" % s, "row", bufs=12)
-            nc.scalar.activation(h2[b, t][:], moist[:], ACT.Tanh)
+            tanhs[b, t] = tile([P, S], F32, "tanh%d" % s, "row%d" % s)
+            nc.scalar.activation(tanhs[b, t][:], moist[:], ACT.Tanh)
 
-        def put(lst, values, gate, b, t):
-            nc.vector.tensor_tensor(pages[b, t][:].indirect(lst[:]), values[:], gate[b, t], ALU.mult)
+        gate2_pairs = [tile([P, 2, S], F32, "gate2_%d" % n) for n in range(4)]
+        gate2 = {(b, t): gate2_pairs[2 * b + t // 2][:, t % 2, :] for b, t in slices}
 
-        put(idx4, h2[0, 0], gate2, 0, 0)
-        put(idx4, h2[0, 1], gate2, 0, 1)
+        def scaled_gate2(b, t, back):
+            nc.scalar.activation(gate2[b, t], back[:], ACT.Copy, scale=gm_sb[:, b, t : t + 1])
+
+        gate2_bank = spread_gate(wg2_rows, "gate2", "big4")
+        gate2_backs = []
+        for t in range(PACK):
+            gate2_backs.append(gate2_bank(t))
+            scaled_gate2(0, t, gate2_backs[t])
+            moist_slice(0, t)
+        for t in range(PACK):
+            scaled_gate2(1, t, gate2_backs[t])
+        gate1_bank = spread_gate(wg1_rows, "gate1", "big5")
+        gate1_backs = [gate1_bank(t) for t in range(PACK)]
+        for t in range(PACK):
+            moist_slice(1, t)
+        gate1 = []
+        for t in range(PACK):
+            gate1.append(tile([P, S], F32, "gate1_%d" % t)[:])
+            nc.scalar.copy(gate1[t], gate1_backs[t][:])
+
+        put(idx4, tanhs[0, 0], gate2[0, 0], 0, 0)
         vw = [gather(tabw[a], idx, U32, "vw%d" % a) for a in range(2)]
         vs = gather(tabs, idx, U8, "vs")
-        for a in range(2):
-            wl_raw[a, 1] = load_weight(wl, a, 1, "wl%d1" % a, "AB"[a])
+        v = [(vw[a][:], vs[LIVE * a :, :]) for a in range(2)]
 
-        sins = {}
+        wl_raw = {}
+        load_page(1, 1)
+        wl_raw[0, 0] = load_weight(wl, 0, 0, "wl00", "big2")
+        load_page(1, 2)
+        wl_raw[1, 0] = load_weight(wl, 1, 0, "wl10", "big3")
+        idx3 = load_list(offs3, "idx3")
+        load_page(1, 3)
+        wcw.append(load_wc(1))
+        wl_raw[0, 1] = load_weight(wl, 0, 1, "wl01", "big0")
+        wl_raw[1, 1] = load_weight(wl, 1, 1, "wl11", "big1")
+        idx5 = load_list(offs5, "idx5")
+        gz_sb = load_factor(gz, "gz_sb")
 
-        def curl_half(g):
-            turns = tile([P, 4, PACK, P], F32, "turns%d" % g, "G")
-            whole = tile([P, 4, PACK, P], F32, "whole%d" % g, "H")
-            for jb in range(4):
-                curl = bank("curl%d%d" % (g, jb))
-                for a in range(2):
-                    nc.tensor.matmul_mx(
-                        out=curl[:],
-                        lhsT=vw[a][:, P * jb : P * (jb + 1)].bitcast(FP8X4),
-                        lhsT_scale=vs[4 * a :, P * jb : P * (jb + 1)],
-                        rhs=wcw[a][:, PASS * g : PASS * (g + 1)].bitcast(FP8X4),
-                        rhs_scale=wcs[4 * a :, PASS * g : PASS * (g + 1)],
-                        start=(a == 0),
-                        stop=(a == 1),
-                    )
+        for b, t in slices[1:]:
+            put(idx4, tanhs[b, t], gate2[b, t], b, t)
+
+        def curl_half(b):
+            turns = tile([P, BLOCKS, PACK, P], F32, "turns%d" % b, "big4")
+            whole = tile([P, BLOCKS, PACK, P], F32, "whole%d" % b, "big5")
+            wc_half = [(wcw[b][:, a, :], wcs[LIVE * a :, PASS * b : PASS * (b + 1)]) for a in range(2)]
+            for jb in range(BLOCKS):
+                curl = bank("curl%d%d" % (b, jb), jb)
+                two_passes(curl, columns(v, jb), wc_half)
                 nc.scalar.activation(
                     turns[:, jb, :, :], curl[:].rearrange("p (m t) -> p t m", t=PACK), ACT.Copy, scale=1.0 / TURN
                 )
-                nearest = tile([P, PACK, P], U32, "nearest%d%d" % (g, jb), "nearest", bufs=2)
+                nearest = tile([P, PACK, P], U32, "nearest%d%d" % (b, jb), "nearest%d" % (jb % 2))
                 nc.scalar.activation(nearest[:], turns[:, jb, :, :], ACT.Copy, bias=ROUND)
                 nc.scalar.activation(whole[:, jb, :, :], nearest[:], ACT.Copy, scale=-1.0, bias=ROUND)
+            return turns, whole
+
+        def slice_bank(b, t):
+            return PACK * (1 - b) + t
+
+        h1 = {}
+
+        def sin_half(b, parts):
             for t in range(PACK):
-                rest = bank("rest%d%d" % (g, t))
-                for jb in range(4):
-                    for n, part in enumerate((turns, whole)):
+                rest = bank("rest%d%d" % (b, t), slice_bank(b, t))
+                for jb in range(BLOCKS):
+                    for n, part in enumerate(parts):
                         nc.tensor.matmul(
                             rest[:, P * jb : P * (jb + 1)], part[:, jb, t, :], ident[:],
                             start=(n == 0), stop=(n == 1), is_transpose=True,
                         )
-                sins[g, t] = tile([P, S], F32, "sin%d%d" % (g, t), "row", bufs=12)
-                nc.scalar.activation(sins[g, t][:], rest[:], ACT.Sin, scale=TURN)
+                h1[b, t] = tile([P, S], F32, "h1_%d%d" % (b, t), "row%d" % (8 * b + t))
+                nc.scalar.activation(h1[b, t][:], rest[:], ACT.Sin, scale=TURN)
 
-        for b, t in slices[2:6]:
-            put(idx4, h2[b, t], gate2, b, t)
+        def shoot_slice(b, t, wlq):
+            shoot = bank("shoot%d%d" % (b, t), slice_bank(b, t))
+            two_passes(shoot, columns(wlq, t), v)
+            nc.vector.tensor_tensor(h1[b, t][:], shoot[:], h1[b, t][:], ALU.min)
+            put(idx3, h1[b, t], gate1[t], b, t)
+
+        def quantize_wl(a, b):
+            n = 2 * b + a
+            return quantize(weave_weight(wl_raw[a, b], "wlb%d" % n, "woven%d" % n), "wlq%d" % n, "q%d" % n)
+
+        def wl_and_sin(b):
+            parts = curl_half(b)
+            wlq = [quantize_wl(0, b)]
+            sin_half(b, parts)
+            wlq.append(quantize_wl(1, b))
+            return wlq
 
         picked = {}
 
-        def shoot_half(g, wlq):
-            for t in range(PACK):
-                shoot = bank("shoot%d%d" % (g, t))
-                for a in range(2):
-                    codes, scales = wlq[a]
-                    nc.tensor.matmul_mx(
-                        out=shoot[:],
-                        lhsT=codes[:, P * t : P * (t + 1)].bitcast(FP8X4),
-                        lhsT_scale=scales[:, P * t : P * (t + 1)],
-                        rhs=vw[a][:].bitcast(FP8X4),
-                        rhs_scale=vs[4 * a :, :],
-                        start=(a == 0),
-                        stop=(a == 1),
-                    )
-                nc.vector.tensor_tensor(sins[g, t][:], shoot[:], sins[g, t][:], ALU.min)
-                put(idx3, sins[g, t], gate1, g, t)
-                if g == 1 and t < 2:
-                    pick(1, t, 0)
-                    pick(1, t, 1)
+        def pick(b, t, h, tag):
+            picked[b, t, h] = tile([P, PASS], F32, "pick%d%d%d" % (b, t, h), tag)
+            width = PASS // 16
+            nc.vector.tensor_copy(picked[b, t, h][:], pages[b, t][:].indirect(idx5[:, width * h : width * (h + 1)]))
 
-        z = {}
+        wlq = wl_and_sin(0)
+        for t in range(PACK):
+            shoot_slice(0, t, wlq)
+        wlq = wl_and_sin(1)
 
-        def pick(b, t, h):
-            picked[b, t, h] = z[b, h][:, t, :]
-            cols = PASS // 16
-            nc.vector.tensor_copy(picked[b, t, h], pages[b, t][:].indirect(idx5[:, cols * h : cols * (h + 1)]))
-
-        wlq = [quantize_weight(wl_raw[a, 0], "wlq%d0" % a, "q%d" % a) for a in range(2)]
-        curl_half(0)
-        shoot_half(0, wlq)
-        for b, t in slices[6:]:
-            put(idx4, h2[b, t], gate2, b, t)
-        wlq = [quantize_weight(wl_raw[a, 1], "wlq%d1" % a, "q%d" % (2 + a)) for a in range(2)]
-        curl_half(1)
-        woq = {}
+        wo_raw = {(b, g): load_weight(wo, b, g, "wo%d%d" % (b, g), "big%d" % (2 + 2 * b + g)) for b in range(2) for g in range(2)}
+        woq = {0: [], 1: []}
+        wo_woven = []
         for b in range(2):
-            for g in range(2):
-                raw = load_weight(wo, b, g, "wo%d%d" % (b, g), "DEAB"[2 * b + g])
-                woq[b, g] = quantize_weight(raw, "woq%d%d" % (b, g), "woq%d%d" % (b, g))
+            woq[0].append(quantize(weave_weight(wo_raw[b, 0], "wob%d0" % b, "woven%d" % (4 + b)), "woq%d" % b, "woq%d" % b))
+            wo_woven.append(weave_weight(wo_raw[b, 1], "wob%d1" % b, "woven%d" % b))
+
+        for t in range(PACK):
+            pick(0, t, 0, "row%d" % t)
+        for t, tag in enumerate(("row4", "row5", "woven2", "woven3")):
+            pick(0, t, 1, tag)
+        for t in range(PACK):
+            shoot_slice(1, t, wlq)
+            if t < 2:
+                pick(1, t, 0, "row%d" % (8 + t))
+                pick(1, t, 1, "gate2_%d" % (2 + t))
+
+        z, x_flat, x_woven = {}, {}, {}
+        xq = {0: [], 1: []}
         for b in range(2):
             for h in range(2):
-                z[b, h] = tile([P, PACK, PASS], F32, "z%d%d" % (b, h), "DEAB"[2 * b + h])
-        for h in range(2):
-            for t in range(PACK):
-                pick(0, t, h)
-        shoot_half(1, wlq)
-        for h in range(2):
-            for t in range(2, PACK):
-                pick(1, t, h)
-
-        xq = {}
-
-        xb = {}
-        for b in range(2):
-            for h in range(2):
-                xb[b, h] = tile([P, PACK, PASS], BF16, "xb%d%d" % (b, h), ("G", "H", "C", "wg2a")[2 * b + h])
+                n = 2 * b + h
+                z[b, h] = tile([P, PACK, PASS], F32, "z%d" % n, "big%d" % (2 + n))
+                x_flat[b, h] = tile([P, PACK, PASS], BF16, "x_flat%d" % n, ("big%d", "gate2_%d")[b] % h)
+                x_woven[b, h] = tile([P, PACK * PASS], BF16, "x_woven%d" % n, "woven%d" % (2 + n))
 
         def absolute(b, t, h):
-            nc.scalar.activation(z[b, h][:, t, :], z[b, h][:, t, :], ACT.Abs)
+            nc.scalar.activation(z[b, h][:, t, :], picked[b, t, h][:], ACT.Abs)
 
-        def scale(b, t, h, out):
-            nc.scalar.activation(out, z[b, h][:, t, :], ACT.Copy, scale=gz_sb[:, b, t : t + 1])
+        def scale(b, t, h):
+            nc.scalar.activation(x_flat[b, h][:, t, :], z[b, h][:, t, :], ACT.Copy, scale=gz_sb[:, b, t : t + 1])
 
         def quantize_x(b, h):
-            grouped = interleave((nc.scalar.copy,), xb[b, h], "xi%d%d" % (b, h))
-            xq[b, h] = quantize(grouped, "xq%d%d" % (b, h), "q%d" % (2 * b + h))
+            xq[h].append(quantize(x_woven[b, h], "xq%d%d" % (b, h), "q%d" % (2 * b + h)))
 
         for h in range(2):
             for t in range(PACK):
                 absolute(0, t, h)
-            if h == 1:
-                quantize_x(0, 0)
             for t in range(PACK):
-                scale(0, t, h, xb[0, h][:, t, :])
-        xi = [tile([P, PACK * PASS], BF16, "xi1%d" % h, "grouped", bufs=4) for h in range(2)]
-
-        def weave(copy, h, ts):
-            copy(
-                out=xi[h][:].rearrange("p (c i t) -> p c t i", t=PACK, i=4)[:, :, ts, :],
-                in_=xb[1, h][:].rearrange("p t (c i) -> p c t i", i=4)[:, :, ts, :],
-            )
-
-        for t in range(2):
+                scale(0, t, h)
+            weave(nc.scalar.copy, x_woven[0, h], x_flat[0, h])
+            quantize_x(0, h)
+        first, last = range(0, 2), range(2, PACK)
+        for t in first:
             for h in range(2):
                 absolute(1, t, h)
-            if t == 0:
-                quantize_x(0, 1)
             for h in range(2):
-                scale(1, t, h, xb[1, h][:, t, :])
+                scale(1, t, h)
         for h in range(2):
-            weave(nc.scalar.copy, h, slice(0, 2))
+            weave(nc.scalar.copy, x_woven[1, h], x_flat[1, h], ts=slice(first.start, first.stop))
+        for t in last:
+            pick(1, t, 0, "row%d" % (8 + t))
+        for t in last:
+            pick(1, t, 1, "row%d" % (2 + t))
         for h in range(2):
-            for t in range(2, PACK):
+            for t in last:
                 absolute(1, t, h)
-            for t in range(2, PACK):
-                scale(1, t, h, xb[1, h][:, t, :])
-            weave(nc.vector.tensor_copy, h, slice(2, PACK))
-            xq[1, h] = quantize(xi[h], "xq1%d" % h, "q%d" % (2 + h))
+            for t in last:
+                scale(1, t, h)
+            weave(nc.scalar.copy, x_woven[1, h], x_flat[1, h], ts=slice(last.start, last.stop))
+            quantize_x(1, h)
+            if h == 0:
+                late_codes = tile([P, 2, PASS], U32, "late_codes", "woven4")
+                for b in range(2):
+                    late_scales = tile([P, PASS], U8, "late_scales%d" % b)
+                    nc.vector.quantize_mx(
+                        out=late_codes[:, b, :].bitcast(FP8X4), scales=late_scales[:], in_=wo_woven[b][:]
+                    )
+                    woq[1].append((late_codes[:, b, :], late_scales[:]))
 
         y_rows = out_0.rearrange("(g p t) j -> g t p j", g=2, t=PACK)
-        y_codes = [tile([P, NJ], U32, "ycodes%d" % g, "wcw%d" % g) for g in range(2)]
-        y_scales = tile([P, 2 * NJ], U8, "yscales", "tabs")
+        y_codes = [tile([P, 2, PASS], U32, "y_codes%d" % h, "wcw%d" % h) for h in range(2)]
+        y_scales = tile([P, 2, 2, PASS], U8, "y_scales", "tabs")
         for h in range(2):
             cols = slice(PASS * h, PASS * (h + 1))
             for g in range(2):
                 for t in range(PACK):
-                    acc = bank("acc%d%d%d" % (h, g, t))
-                    for b in range(2):
-                        nc.tensor.matmul_mx(
-                            out=acc[:],
-                            lhsT=woq[b, g][0][:, P * t : P * (t + 1)].bitcast(FP8X4),
-                            lhsT_scale=woq[b, g][1][:, P * t : P * (t + 1)],
-                            rhs=xq[b, h][0][:].bitcast(FP8X4),
-                            rhs_scale=xq[b, h][1][:],
-                            start=(b == 0),
-                            stop=(b == 1),
-                        )
+                    acc = bank("acc%d%d%d" % (h, g, t), slice_bank(g, t))
+                    two_passes(acc, columns(woq[g], t), xq[h])
                     y = z[g, h][:, t, :]
                     nc.vector.tensor_tensor(y, acc[:], y, ALU.add)
                     nc.sync.dma_start(y_rows[g, t][:, cols], y)
-                shares = (nc.scalar.copy, nc.vector.tensor_copy) if (g, h) == (1, 1) else (nc.scalar.copy,)
-                grouped = interleave(shares, z[g, h], "yi%d%d" % (g, h))
+                y_woven = tile([P, PACK * PASS], BF16, "y_woven%d%d" % (g, h), "woven%d" % (2 * h + g))
+                if (g, h) == (1, 1):
+                    weave(nc.scalar.copy, y_woven, z[g, h], runs=slice(0, SCALAR_RUNS))
+                    weave(nc.vector.tensor_copy, y_woven, z[g, h], runs=slice(SCALAR_RUNS, PASS // RUN))
+                else:
+                    weave(nc.scalar.copy, y_woven, z[g, h])
                 nc.vector.quantize_mx(
-                    out=y_codes[g][:, cols].bitcast(FP8X4),
-                    scales=y_scales[:, NJ * g + PASS * h : NJ * g + PASS * (h + 1)],
-                    in_=grouped[:],
+                    out=y_codes[h][:, g, :].bitcast(FP8X4), scales=y_scales[:, h, g, :], in_=y_woven[:]
                 )
+                nc.sync.dma_start(as_words(out_1[g])[:, cols], y_codes[h][:, g, :].bitcast(I32))
+            for r in range(LIVE):
                 nc.sync.dma_start(
-                    out_1[g].rearrange("p m t -> p (m t)").bitcast(I32)[:, cols], y_codes[g][:, cols].bitcast(I32)
+                    out_2[:, r : LIVE * QUADS : LIVE, cols].bitcast(I32).rearrange("g q m -> q g m"),
+                    y_scales[r:P:QUAD, h].bitcast(I32),
                 )
-        for q in range(QUADS):
-            nc.sync.dma_start(
-                out_2.bitcast(I32)[:, 4 * q : 4 * q + 4, :].rearrange("g r m -> r g m"),
-                y_scales[32 * q : 32 * q + 4, :].bitcast(I32).rearrange("r (g m) -> r g m", g=2),
-            )

import math
from contextlib import ExitStack

import concourse.mybir as mybir
from concourse.masks import make_identity

S, T2, NJ, K, K2, H = 512, 2048, 1024, 1024, 512, 1024
FLOPS = 2 * K * H * S * 2 + 2 * K2 * H * S + 2 * H * H * NJ

F32 = mybir.dt.float32
BF16 = mybir.dt.bfloat16
I32 = mybir.dt.int32
U32 = mybir.dt.uint32
U16 = mybir.dt.uint16
U8 = mybir.dt.uint8
FP8X4 = mybir.dt.float8_e4m3fn_x4
FP4X4 = mybir.dt.float4_e2m1fn_x4
ACT = mybir.ActivationFunctionType
ALU = mybir.AluOpType

P = 128
PACK = 4
PASS = P * PACK
QUAD = 32
QUADS = P // QUAD
LIVE = 4
BLOCKS = S // P
RUN = 4
TURN = 2.0 * math.pi
ROUND = 1.5 * 2.0**23
SCALAR_RUNS = 48


def tile_list_bonsai_branch_slots_kernel(
    tc, tab_words, tab_scales, tab2_words, tab2_scales, offs, offs2, offs3, offs4, offs5,
    wl, wc_words, wc_scales, wm_words, wm_scales, gm, wg1, wg2, page0, gz, wo,
    out_0, out_1, out_2,
):
    nc = tc.nc
    slices = [(b, t) for b in range(2) for t in range(PACK)]

    with ExitStack() as ctx:
        lists = ctx.enter_context(tc.tile_pool(name="lists", bufs=1))
        sb = ctx.enter_context(tc.tile_pool(name="sb", bufs=1))
        psum = ctx.enter_context(tc.psum_pool(name="psum", bufs=1))

        def tile(shape, dtype, name, tag=None):
            return sb.tile(shape, dtype, name=name, tag=tag or name, align_bytes=64)

        def bank(name, n):
            return psum.tile([P, PASS], F32, name=name, tag="bank%d" % n)

        def load_list(src, name):
            lst = lists.tile(list(src.shape), U16, name=name)
            nc.sync.dma_start(lst[:], src)
            return lst

        def load(src, dtype, name, tag=None):
            dst = tile(list(src.shape), dtype, name, tag)
            nc.sync.dma_start(dst[:], src)
            return dst

        def as_words(src):
            return src.rearrange("p n i -> p (n i)").bitcast(I32)

        def zeroed_planes(src, name):
            dst = tile([P, src.shape[2]], U8, name)
            nc.gpsimd.memset(dst[:].bitcast(I32), 0)
            return dst

        def load_plane(dst, src):
            for r in range(LIVE):
                nc.sync.dma_start(dst[r:P:QUAD, :].bitcast(I32), src[0, r : LIVE * QUADS : LIVE, :].bitcast(I32))

        def load_two_planes(src, name):
            dst = zeroed_planes(src, name)
            for quad in range(QUADS):
                nc.sync.dma_start(
                    dst[QUAD * quad : QUAD * quad + 2 * LIVE, :].bitcast(I32),
                    src[:, LIVE * quad : LIVE * (quad + 1), :].bitcast(I32),
                )
            return dst

        def load_factor(src, name):
            return load(src.rearrange("(b p t) -> p b t", b=2, t=PACK), F32, name)

        page_rows = page0.rearrange("(b p t) c -> b t p c", b=2, t=PACK)
        pages = {}

        def load_page(b, t):
            pages[b, t] = load(page_rows[b, t], F32, "page%d%d" % (b, t))

        def load_weight(src, a, g, name, tag):
            rows = src[PASS * a : PASS * (a + 1), PASS * g : PASS * (g + 1)]
            return load(rows.rearrange("(p i) c -> p i c", i=PACK), F32, name, tag)

        def load_wc(g):
            words = wc_words.rearrange("a p n i -> p a (n i)").bitcast(I32)
            return load(words[:, :, PASS * g : PASS * (g + 1)], I32, "wcw%d" % g)

        def gather(window, lst, dtype, name):
            picked = tile([P, S], dtype, name)
            nc.vector.tensor_copy(picked[:], window[:].bitcast(dtype).indirect(lst[:]))
            return picked

        def quantize(woven, name, tag):
            codes = tile([P, PASS], U32, name, tag)
            scales = tile([P, PASS], U8, name + "s", tag + "s")
            nc.vector.quantize_mx(out=codes[:].bitcast(FP8X4), scales=scales[:], in_=woven[:])
            return codes[:], scales[:]

        def weave_weight(raw, name, tag):
            woven = tile([P, PACK * PASS], BF16, name, tag)
            nc.scalar.copy(
                out=woven[:].rearrange("p (t m i) -> p m t i", t=PACK, i=PACK),
                in_=raw[:].rearrange("p i (m t) -> p m t i", t=PACK),
            )
            return woven

        def weave(copy, woven, src, runs=slice(0, PASS // RUN), ts=slice(0, PACK)):
            copy(
                out=woven[:].rearrange("p (u e t) -> p u t e", t=PACK, e=RUN)[:, runs, ts, :],
                in_=src[:].rearrange("p t (u e) -> p u t e", e=RUN)[:, runs, ts, :],
            )

        def two_passes(out, stationary, moving):
            for a in range(2):
                nc.tensor.matmul_mx(
                    out=out[:],
                    lhsT=stationary[a][0].bitcast(FP8X4),
                    lhsT_scale=stationary[a][1],
                    rhs=moving[a][0].bitcast(FP8X4),
                    rhs_scale=moving[a][1],
                    start=(a == 0),
                    stop=(a == 1),
                )

        def columns(operand, n):
            return [(codes[:, P * n : P * (n + 1)], scales[:, P * n : P * (n + 1)]) for codes, scales in operand]

        def spread_gate(rows, name, tag):
            turned = bank(name + "_turned", 7)
            for jb in range(BLOCKS):
                nc.tensor.transpose(turned[:, P * jb : P * (jb + 1)], rows[:, P * jb : P * (jb + 1)], ident[:])
            repeated = tile([P, PACK, BLOCKS, QUADS, QUAD], F32, name + "_repeated", tag)
            by_t = turned[:].rearrange("p (jb m t) -> p t jb m", jb=BLOCKS, t=PACK)

            def gate_bank(t):
                nc.scalar.copy(repeated[:, t], by_t[:, t].unsqueeze(2).to_broadcast([P, BLOCKS, QUADS, QUAD]))
                back = bank("%s_back%d" % (name, t), 3 + t)
                for jb in range(BLOCKS):
                    nc.tensor.transpose(
                        back[:, P * jb : P * (jb + 1)], repeated[:, t, jb].rearrange("p q m -> p (q m)"), ident[:]
                    )
                return back

            return gate_bank

        def put(lst, values, gate, b, t):
            nc.vector.tensor_tensor(pages[b, t][:].indirect(lst[:]), values[:], gate, ALU.mult)

        warm = tile([P, 8], F32, "warm")
        nc.vector.memset(warm[:], 0.0)
        nc.scalar.activation(warm[:], warm[:], ACT.Silu)

        wg2_rows = load(wg2, F32, "wg2_rows", "nearest0")
        idx2 = load_list(offs2, "idx2")
        tab2s = zeroed_planes(tab2_scales, "tab2s")
        load_plane(tab2s, tab2_scales)
        wm_raw = tile([P, 2 * H], U8, "wm_raw")
        nc.sync.dma_start(wm_raw[:].bitcast(I32), wm_words[0].bitcast(I32))
        tab2w = load(as_words(tab2_words[0]), I32, "tab2w", "big2")
        wms_raw = zeroed_planes(wm_scales, "wms_raw")
        load_plane(wms_raw, wm_scales)
        gm_sb = load_factor(gm, "gm_sb")
        idx4 = load_list(offs4, "idx4")
        load_page(0, 0)
        load_page(0, 1)
        wg1_rows = load(wg1, F32, "wg1_rows", "nearest1")
        idx = load_list(offs, "idx")
        tabs = load_two_planes(tab_scales, "tabs")
        tabw = [load(as_words(tab_words[a]), I32, "tabw%d" % a, "big%d" % a) for a in range(2)]
        load_page(0, 2)
        wcw = [load_wc(0)]
        wcs = load_two_planes(wc_scales, "wcs")
        load_page(0, 3)
        load_page(1, 0)
        ident = tile([P, P], F32, "ident")
        make_identity(nc, ident[:])

        v2s = gather(tab2s, idx2, U8, "v2s")
        wm_dealt = tile([P, 2 * H], U8, "wm_dealt")
        nc.vector.tensor_copy(
            wm_dealt[:].bitcast(U16).rearrange("p (b t m) -> p b t m", b=2, t=PACK),
            wm_raw[:].bitcast(U16).rearrange("p (b m t) -> p b t m", b=2, t=PACK),
        )
        v2w = gather(tab2w, idx2, U32, "v2w")
        wms_dealt = tile([P, H], U8, "wms_dealt")
        for b in range(2):
            nc.vector.tensor_copy(
                wms_dealt[:].rearrange("p (b t m) -> p b t m", b=2, t=PACK)[:, b],
                wms_raw[:].rearrange("p (b m t) -> p b t m", b=2, t=PACK)[:, b],
            )

        tanhs = {}

        def moist_slice(b, t):
            s = PACK * b + t
            moist = bank("moist%d" % s, s % 3)
            nc.tensor.matmul_mx(
                out=moist[:],
                lhsT=wm_dealt[:, 2 * P * s : 2 * P * (s + 1)].bitcast(FP4X4),
                lhsT_scale=wms_dealt[:, P * s : P * (s + 1)],
                rhs=v2w[:].bitcast(FP8X4),
                rhs_scale=v2s[:],
                start=True,
                stop=True,
            )
            tanhs[b, t] = tile([P, S], F32, "tanh%d" % s, "row%d" % s)
            nc.scalar.activation(tanhs[b, t][:], moist[:], ACT.Tanh)

        gate2_pairs = [tile([P, 2, S], F32, "gate2_%d" % n) for n in range(4)]
        gate2 = {(b, t): gate2_pairs[2 * b + t // 2][:, t % 2, :] for b, t in slices}

        def scaled_gate2(b, t, back):
            nc.scalar.activation(gate2[b, t], back[:], ACT.Copy, scale=gm_sb[:, b, t : t + 1])

        gate2_bank = spread_gate(wg2_rows, "gate2", "big4")
        gate2_backs = []
        for t in range(PACK):
            gate2_backs.append(gate2_bank(t))
            scaled_gate2(0, t, gate2_backs[t])
            moist_slice(0, t)
        for t in range(PACK):
            scaled_gate2(1, t, gate2_backs[t])
        gate1_bank = spread_gate(wg1_rows, "gate1", "big5")
        gate1_backs = [gate1_bank(t) for t in range(PACK)]
        for t in range(PACK):
            moist_slice(1, t)
        gate1 = []
        for t in range(PACK):
            gate1.append(tile([P, S], F32, "gate1_%d" % t)[:])
            nc.scalar.copy(gate1[t], gate1_backs[t][:])

        put(idx4, tanhs[0, 0], gate2[0, 0], 0, 0)
        vw = [gather(tabw[a], idx, U32, "vw%d" % a) for a in range(2)]
        vs = gather(tabs, idx, U8, "vs")
        v = [(vw[a][:], vs[LIVE * a :, :]) for a in range(2)]

        wl_raw = {}
        load_page(1, 1)
        wl_raw[0, 0] = load_weight(wl, 0, 0, "wl00", "big2")
        load_page(1, 2)
        wl_raw[1, 0] = load_weight(wl, 1, 0, "wl10", "big3")
        idx3 = load_list(offs3, "idx3")
        load_page(1, 3)
        wcw.append(load_wc(1))
        wl_raw[0, 1] = load_weight(wl, 0, 1, "wl01", "big0")
        wl_raw[1, 1] = load_weight(wl, 1, 1, "wl11", "big1")
        idx5 = load_list(offs5, "idx5")
        gz_sb = load_factor(gz, "gz_sb")

        for b, t in slices[1:]:
            put(idx4, tanhs[b, t], gate2[b, t], b, t)

        def curl_half(b):
            turns = tile([P, BLOCKS, PACK, P], F32, "turns%d" % b, "big4")
            whole = tile([P, BLOCKS, PACK, P], F32, "whole%d" % b, "big5")
            wc_half = [(wcw[b][:, a, :], wcs[LIVE * a :, PASS * b : PASS * (b + 1)]) for a in range(2)]
            for jb in range(BLOCKS):
                curl = bank("curl%d%d" % (b, jb), jb)
                two_passes(curl, columns(v, jb), wc_half)
                nc.scalar.activation(
                    turns[:, jb, :, :], curl[:].rearrange("p (m t) -> p t m", t=PACK), ACT.Copy, scale=1.0 / TURN
                )
                nearest = tile([P, PACK, P], U32, "nearest%d%d" % (b, jb), "nearest%d" % (jb % 2))
                nc.scalar.activation(nearest[:], turns[:, jb, :, :], ACT.Copy, bias=ROUND)
                nc.scalar.activation(whole[:, jb, :, :], nearest[:], ACT.Copy, scale=-1.0, bias=ROUND)
            return turns, whole

        def slice_bank(b, t):
            return PACK * (1 - b) + t

        h1 = {}

        def sin_half(b, parts):
            for t in range(PACK):
                rest = bank("rest%d%d" % (b, t), slice_bank(b, t))
                for jb in range(BLOCKS):
                    for n, part in enumerate(parts):
                        nc.tensor.matmul(
                            rest[:, P * jb : P * (jb + 1)], part[:, jb, t, :], ident[:],
                            start=(n == 0), stop=(n == 1), is_transpose=True,
                        )
                h1[b, t] = tile([P, S], F32, "h1_%d%d" % (b, t), "row%d" % (8 * b + t))
                nc.scalar.activation(h1[b, t][:], rest[:], ACT.Sin, scale=TURN)

        def shoot_slice(b, t, wlq):
            shoot = bank("shoot%d%d" % (b, t), slice_bank(b, t))
            two_passes(shoot, columns(wlq, t), v)
            nc.vector.tensor_tensor(h1[b, t][:], shoot[:], h1[b, t][:], ALU.min)
            put(idx3, h1[b, t], gate1[t], b, t)

        def quantize_wl(a, b):
            n = 2 * b + a
            return quantize(weave_weight(wl_raw[a, b], "wlb%d" % n, "woven%d" % n), "wlq%d" % n, "q%d" % n)

        def wl_and_sin(b):
            parts = curl_half(b)
            wlq = [quantize_wl(0, b)]
            sin_half(b, parts)
            wlq.append(quantize_wl(1, b))
            return wlq

        picked = {}

        def pick(b, t, h, tag):
            picked[b, t, h] = tile([P, PASS], F32, "pick%d%d%d" % (b, t, h), tag)
            width = PASS // 16
            nc.vector.tensor_copy(picked[b, t, h][:], pages[b, t][:].indirect(idx5[:, width * h : width * (h + 1)]))

        wlq = wl_and_sin(0)
        for t in range(PACK):
            shoot_slice(0, t, wlq)
        wlq = wl_and_sin(1)

        wo_raw = {(b, g): load_weight(wo, b, g, "wo%d%d" % (b, g), "big%d" % (2 + 2 * b + g)) for b in range(2) for g in range(2)}
        woq = {0: [], 1: []}
        wo_woven = []
        for b in range(2):
            woq[0].append(quantize(weave_weight(wo_raw[b, 0], "wob%d0" % b, "woven%d" % (4 + b)), "woq%d" % b, "woq%d" % b))
            wo_woven.append(weave_weight(wo_raw[b, 1], "wob%d1" % b, "woven%d" % b))

        for t in range(PACK):
            pick(0, t, 0, "row%d" % t)
        for t, tag in enumerate(("row4", "row5", "woven2", "woven3")):
            pick(0, t, 1, tag)
        for t in range(PACK):
            shoot_slice(1, t, wlq)
            if t < 2:
                pick(1, t, 0, "row%d" % (8 + t))
                pick(1, t, 1, "gate2_%d" % (2 + t))

        z, x_flat, x_woven = {}, {}, {}
        xq = {0: [], 1: []}
        for b in range(2):
            for h in range(2):
                n = 2 * b + h
                z[b, h] = tile([P, PACK, PASS], F32, "z%d" % n, "big%d" % (2 + n))
                x_flat[b, h] = tile([P, PACK, PASS], BF16, "x_flat%d" % n, ("big%d", "gate2_%d")[b] % h)
                x_woven[b, h] = tile([P, PACK * PASS], BF16, "x_woven%d" % n, "woven%d" % (2 + n))

        def absolute(b, t, h):
            nc.scalar.activation(z[b, h][:, t, :], picked[b, t, h][:], ACT.Abs)

        def scale(b, t, h):
            nc.scalar.activation(x_flat[b, h][:, t, :], z[b, h][:, t, :], ACT.Copy, scale=gz_sb[:, b, t : t + 1])

        def quantize_x(b, h):
            xq[h].append(quantize(x_woven[b, h], "xq%d%d" % (b, h), "q%d" % (2 * b + h)))

        for h in range(2):
            for t in range(PACK):
                absolute(0, t, h)
            for t in range(PACK):
                scale(0, t, h)
            weave(nc.scalar.copy, x_woven[0, h], x_flat[0, h])
            quantize_x(0, h)
        first, last = range(0, 2), range(2, PACK)
        for t in first:
            for h in range(2):
                absolute(1, t, h)
            for h in range(2):
                scale(1, t, h)
        for h in range(2):
            weave(nc.scalar.copy, x_woven[1, h], x_flat[1, h], ts=slice(first.start, first.stop))
        for t in last:
            pick(1, t, 0, "row%d" % (8 + t))
        for t in last:
            pick(1, t, 1, "row%d" % (2 + t))
        for h in range(2):
            for t in last:
                absolute(1, t, h)
            for t in last:
                scale(1, t, h)
            weave(nc.scalar.copy, x_woven[1, h], x_flat[1, h], ts=slice(last.start, last.stop))
            quantize_x(1, h)
            if h == 0:
                late_codes = tile([P, 2, PASS], U32, "late_codes", "woven4")
                for b in range(2):
                    late_scales = tile([P, PASS], U8, "late_scales%d" % b)
                    nc.vector.quantize_mx(
                        out=late_codes[:, b, :].bitcast(FP8X4), scales=late_scales[:], in_=wo_woven[b][:]
                    )
                    woq[1].append((late_codes[:, b, :], late_scales[:]))

        y_rows = out_0.rearrange("(g p t) j -> g t p j", g=2, t=PACK)
        y_codes = [tile([P, 2, PASS], U32, "y_codes%d" % h, "wcw%d" % h) for h in range(2)]
        y_scales = tile([P, 2, 2, PASS], U8, "y_scales", "tabs")
        for h in range(2):
            cols = slice(PASS * h, PASS * (h + 1))
            for g in range(2):
                for t in range(PACK):
                    acc = bank("acc%d%d%d" % (h, g, t), slice_bank(g, t))
                    two_passes(acc, columns(woq[g], t), xq[h])
                    y = z[g, h][:, t, :]
                    nc.vector.tensor_tensor(y, acc[:], y, ALU.add)
                    nc.sync.dma_start(y_rows[g, t][:, cols], y)
                y_woven = tile([P, PACK * PASS], BF16, "y_woven%d%d" % (g, h), "woven%d" % (2 * h + g))
                if (g, h) == (1, 1):
                    weave(nc.scalar.copy, y_woven, z[g, h], runs=slice(0, SCALAR_RUNS))
                    weave(nc.vector.tensor_copy, y_woven, z[g, h], runs=slice(SCALAR_RUNS, PASS // RUN))
                else:
                    weave(nc.scalar.copy, y_woven, z[g, h])
                nc.vector.quantize_mx(
                    out=y_codes[h][:, g, :].bitcast(FP8X4), scales=y_scales[:, h, g, :], in_=y_woven[:]
                )
                nc.sync.dma_start(as_words(out_1[g])[:, cols], y_codes[h][:, g, :].bitcast(I32))
            for r in range(LIVE):
                nc.sync.dma_start(
                    out_2[:, r : LIVE * QUADS : LIVE, cols].bitcast(I32).rearrange("g q m -> q g m"),
                    y_scales[r:P:QUAD, h].bitcast(I32),
                )
